import numpy as np
import ml_dtypes


def mxq(x, axis, fmt="e4m3"):
    dtype, down = {"e4m3": (ml_dtypes.float8_e4m3fn, 7), "e5m2": (ml_dtypes.float8_e5m2, 14)}[fmt]
    v = np.moveaxis(np.asarray(x, np.float32).astype(ml_dtypes.bfloat16).astype(np.float64), axis, -1)
    blocks = v.reshape(v.shape[:-1] + (-1, 32))
    amax = np.abs(blocks).max(-1, keepdims=True)
    byte = np.maximum(np.where(amax > 0, np.frexp(amax)[1] - 1 + 127, 0) - down, 1)
    scale = np.exp2(byte - 127.0)
    codes = (blocks / scale).astype(np.float32).astype(dtype).astype(np.float64)
    return np.moveaxis((codes * scale).reshape(v.shape), -1, axis)


WIDE = False


def mx_kscale(k):
    if not WIDE:
        return np.ones(k)
    levels = np.array([10, -10, 5, -5, 0])
    if k % 512:
        return np.exp2(np.random.permutation(np.resize(levels, k // 32))).repeat(32)
    a = np.empty((k // 512, 16))
    for p in range(k // 512):
        a[p, :8] = np.random.permutation(np.resize(levels, 8))
        for g in range(8):
            far = levels[np.abs(levels - a[p, g]) >= 10]
            a[p, g + 8] = far[np.random.randint(len(far))]
    return np.exp2(a.ravel()).repeat(32)


def f64(x):
    return np.asarray(x).astype(np.float64)


def striped(idx):
    return np.tile(idx.reshape(-1, 16).T, (8, 1)).astype(np.uint16)


def unstriped(offs):
    return offs[:16].T.reshape(-1).astype(np.int64)


def pack_weight(w):
    k, n = w.shape
    w = f64(np.asarray(w, np.float32).astype(ml_dtypes.bfloat16)).reshape(k // 32, 32, n)
    amax = np.abs(w).max(1)
    byte = np.clip(np.where(amax > 0, np.frexp(amax)[1] - 1 + 127 - 7, 1), 1, 254)
    scaled = (w * np.exp2(127.0 - byte)[:, None, :]).reshape(k, n).astype(np.float32)
    words = np.ascontiguousarray(scaled.reshape(k // 512, 128, 4, n).transpose(0, 1, 3, 2)).astype(ml_dtypes.float8_e4m3fn).view(np.uint8)
    return words, np.ascontiguousarray(byte.astype(np.uint8).reshape(k // 512, 16, n))


def unpack_weight(words, scales):
    g, p, n, _ = words.shape
    vals = np.ascontiguousarray(words).view(ml_dtypes.float8_e4m3fn).astype(np.float64) * np.repeat(np.exp2(scales.astype(np.float64) - 127.0), 8, axis=1)[..., None]
    return vals.transpose(0, 1, 3, 2).reshape(g * 512, n)


def sigmoid(v):
    return 1.0 / (1.0 + np.exp(-np.maximum(v, -700.0)))


K, T, S, D, N, V = 512, 4096, 1024, 4, 128, 256
P = 2 ** 7


def setup_inputs():
    n = np.random.standard_normal
    s = mx_kscale(K)[:, None]
    packed_xT = pack_weight(n((K, T)) * s)
    return {
        "x_words": packed_xT[0],
        "x_scales": packed_xT[1],
        "w1": (n((K, N)) / np.sqrt(K) / s).astype(np.float32),
        "w2": (n((K, N)) / np.sqrt(K) / s).astype(np.float32),
        "delay": (np.tile(np.random.uniform(0.1, 2.0, V), (P, 1))).astype(np.float32),
        "elapsed": (np.tile(np.random.uniform(0.1, 2.0, V), (P, 1))).astype(np.float32),
        "seen": ((np.random.uniform(size=(N, V)) < 0.3) * 1.0).astype(np.float32),
        "offs": striped(np.random.permutation(T)[:S]),
    }


def reference(x_words, x_scales, w1, w2, delay, elapsed, seen, offs):
    xq = unpack_weight(x_words, x_scales)[:, unstriped(offs)]
    y = mxq(f64(w1), 0, "e4m3").T @ xq
    a = y.reshape(len(y), -1, D).mean(axis=2)
    p = sigmoid(a)
    h = mxq(f64(w2), 0, "e4m3").T @ xq
    lh = h.reshape(len(h), -1, D).mean(axis=2)
    lam = np.exp(lh)
    ln = np.log(p * (np.exp(-1.0 * (lam * f64(elapsed)[:1])) - 1.0) + 1.0)
    lp = np.log(p) + lh - (lam * f64(delay)[:1])
    return np.exp(ln + f64(seen) * (lp - ln))

@@ -1,0 +1,153 @@
+from contextlib import ExitStack
+
+import concourse.mybir as mybir
+from concourse.masks import make_identity
+
+F32 = mybir.dt.float32
+BF16 = mybir.dt.bfloat16
+I32 = mybir.dt.int32
+U32 = mybir.dt.uint32
+U16 = mybir.dt.uint16
+U8 = mybir.dt.uint8
+FP8X4 = mybir.dt.float8_e4m3fn_x4
+ALU = mybir.AluOpType
+ACT = mybir.ActivationFunctionType
+
+P = 128
+K, T, S, D, N, V = 512, 4096, 1024, 4, 128, 256
+PACK = 4
+PIECES = 2
+PV = V // PIECES
+PS = S // PIECES
+
+FLOPS = 2 * 2 * K * N * S
+
+
+def tile_picked_ydfm_lik_p_kernel(tc, x_words, x_scales, w1, w2, delay, elapsed, seen, offs, out):
+    nc = tc.nc
+    with ExitStack() as ctx:
+        keep = ctx.enter_context(tc.tile_pool(name="keep", bufs=1))
+        psum = ctx.enter_context(tc.psum_pool(name="psum", bufs=1))
+
+        offsets = keep.tile([P, S // 16], U16, name="offsets")
+        nc.sync.dma_start(offsets[:], offs)
+
+        scale_table = keep.tile([P, T], U8, name="scale_table", align_bytes=64)
+        nc.gpsimd.memset(scale_table[:, : T // 2].bitcast(I32), 0)
+        nc.vector.memset(scale_table[:, T // 2 :].bitcast(I32), 0)
+        nc.scalar.dma_start(scale_table[32:96:4, :].bitcast(I32), x_scales[0].bitcast(I32))
+        x_plane = keep.tile([P, S], U8, name="x_plane", align_bytes=64)
+        nc.vector.memset(x_plane[:].bitcast(I32), 0)
+
+        delay_col = keep.tile([P, 2], F32, name="delay_col")
+        elapsed_col = keep.tile([P, 2], F32, name="elapsed_col")
+        nc.sync.dma_start(delay_col[:], delay[0].rearrange("(p j) -> p j", j=2))
+        nc.sync.dma_start(elapsed_col[:], elapsed[0].rearrange("(p j) -> p j", j=2))
+        seen_sb = keep.tile([P, V], F32, name="seen_sb")
+        nc.sync.dma_start(seen_sb[:], seen)
+
+        w2_raw = keep.tile([P, PACK, N], F32, name="w2_raw")
+        nc.sync.dma_start(w2_raw[:], w2.rearrange("(p j) n -> p j n", j=PACK))
+        w1_raw = keep.tile([P, PACK, N], F32, name="w1_raw")
+        nc.sync.dma_start(w1_raw[:], w1.rearrange("(p j) n -> p j n", j=PACK))
+        word_table = keep.tile([P, T], I32, name="word_table", align_bytes=64)
+        nc.sync.dma_start(word_table[:], x_words[0].rearrange("p c r -> p (c r)").bitcast(I32))
+
+        ident = keep.tile([P, P], F32, name="ident")
+        make_identity(nc, ident[:])
+
+        warm = keep.tile([P, 1], F32, name="warm")
+        nc.scalar.activation(warm[:], delay_col[:, 0:1], ACT.Exp, scale=-1.0)
+
+        picked_scales = keep.tile([P, S], U8, name="picked_scales", align_bytes=64)
+        nc.vector.tensor_copy(picked_scales[:], scale_table[:].indirect(offsets[:]))
+        dealt_scales = keep.tile([P, S], U8, name="dealt_scales", align_bytes=64)
+        nc.vector.tensor_copy(
+            dealt_scales[:].rearrange("p (h d v) -> p h d v", h=PIECES, d=D),
+            picked_scales[:].rearrange("p (h v d) -> p h d v", h=PIECES, d=D),
+        )
+        for i in range(4):
+            nc.sync.dma_start(x_plane[i:P:32, :].bitcast(I32), dealt_scales[32 + 4 * i : 96 : 16, :].bitcast(I32))
+
+        neg_elapsed_col = keep.tile([P, 2], F32, name="neg_elapsed_col")
+        nc.scalar.mul(neg_elapsed_col[:], elapsed_col[:], -1.0)
+        seen_t = psum.tile([P, 2, P], F32, name="seen_t")
+        for j in range(2):
+            nc.tensor.transpose(seen_t[:, j, :], seen_sb[:, j:V:2], ident[:])
+        seen_delay = keep.tile([P, 2, P], F32, name="seen_delay")
+        unseen_elapsed = keep.tile([P, 2, P], F32, name="unseen_elapsed")
+        t_ps = psum.tile([P, 2, P], F32, name="t_ps")
+        for j in range(2):
+            nc.scalar.activation(seen_delay[:, j, :], seen_t[:, j, :], ACT.Copy, scale=delay_col[:, j : j + 1])
+            nc.scalar.activation(
+                unseen_elapsed[:, j, :], seen_t[:, j, :], ACT.Identity,
+                scale=neg_elapsed_col[:, j : j + 1], bias=elapsed_col[:, j : j + 1],
+            )
+        for j in range(2):
+            nc.tensor.matmul(t_ps[:, j, :], seen_delay[:, j, :], ident[:], start=True, stop=False, is_transpose=True)
+            nc.tensor.matmul(t_ps[:, j, :], unseen_elapsed[:, j, :], ident[:], start=False, stop=True, is_transpose=True)
+        neg_half_unseen = keep.tile([P, V], F32, name="neg_half_unseen")
+        nc.scalar.activation(neg_half_unseen[:], seen_sb[:], ACT.Copy, scale=0.5, bias=-0.5)
+
+        def quantize(raw, name):
+            grouped = keep.tile([P, N, PACK], BF16, name=name + "_grouped", align_bytes=64)
+            codes = keep.tile([P, N], U32, name=name + "_codes", align_bytes=64)
+            scales = keep.tile([P, N], U8, name=name + "_scales", align_bytes=64)
+            nc.scalar.copy(
+                grouped[:].rearrange("p (c i) t -> p c t i", i=4), raw[:].rearrange("p t (c i) -> p c t i", i=4)
+            )
+            nc.vector.quantize_mx(codes[:].bitcast(FP8X4), scales[:], grouped[:].rearrange("p n t -> p (n t)"))
+            return codes, scales
+
+        w2_q = quantize(w2_raw, "w2")
+        w1_q = quantize(w1_raw, "w1")
+
+        picked = []
+        for h in range(PIECES):
+            words = keep.tile([P, D, PV], U32, name="picked_words%d" % h, align_bytes=64)
+            cols = slice(h * PS // 16, (h + 1) * PS // 16)
+            nc.vector.tensor_copy(words[:].rearrange("p d v -> p v d"), word_table[:].bitcast(U32).indirect(offsets[:, cols]))
+            picked.append(words)
+
+        def product(w_q, h, name):
+            acc = psum.tile([P, PV], F32, name=name)
+            for d in range(D):
+                nc.tensor.matmul_mx(
+                    acc[:],
+                    lhsT=w_q[0][:].bitcast(FP8X4),
+                    lhsT_scale=w_q[1][:],
+                    rhs=picked[h][:, d, :].bitcast(FP8X4),
+                    rhs_scale=x_plane[:, (h * D + d) * PV : (h * D + d + 1) * PV],
+                    start=(d == 0),
+                    stop=(d == D - 1),
+                )
+            return acc
+
+        h_sum, y_sum = [], []
+        for h in range(PIECES):
+            h_sum.append(product(w2_q, h, "h_sum%d" % h))
+            y_sum.append(product(w1_q, h, "y_sum%d" % h))
+
+        def tiles(name):
+            return [keep.tile([P, PV], F32, name="%s%d" % (name, h)) for h in range(PIECES)]
+
+        lam, seen_lh, decay, z, e, th, q, r, res = [
+            tiles(n) for n in ("lam", "seen_lh", "decay", "z", "e", "th", "q", "r", "res")
+        ]
+        vs = [slice(h * PV, (h + 1) * PV) for h in range(PIECES)]
+        for h in range(PIECES):
+            nc.scalar.activation(lam[h][:], h_sum[h][:], ACT.Exp, scale=1.0 / D)
+            nc.vector.scalar_tensor_tensor(seen_lh[h][:], h_sum[h][:], 1.0 / D, seen_sb[:, vs[h]], ALU.mult, ALU.mult)
+            nc.scalar.activation(th[h][:], y_sum[h][:], ACT.Tanh, scale=0.5 / D)
+            nc.vector.tensor_tensor(
+                decay[h][:].rearrange("m (p j) -> m p j", j=2),
+                t_ps[:, :, h * PV // 2 : (h + 1) * PV // 2].rearrange("m j p -> m p j"),
+                lam[h][:].rearrange("m (p j) -> m p j", j=2),
+                ALU.mult,
+            )
+            nc.vector.tensor_tensor(z[h][:], seen_lh[h][:], decay[h][:], ALU.subtract)
+            nc.scalar.activation(e[h][:], z[h][:], ACT.Exp)
+            nc.vector.scalar_tensor_tensor(q[h][:], th[h][:], -1.0, neg_half_unseen[:, vs[h]], ALU.add, ALU.mult)
+            nc.vector.scalar_tensor_tensor(r[h][:], th[h][:], 1.0, e[h][:], ALU.add, ALU.mult)
+            nc.vector.scalar_tensor_tensor(res[h][:], r[h][:], 0.5, q[h][:], ALU.mult, ALU.add)
+            nc.sync.dma_start(out[:, vs[h]], res[h][:])

@@ -33,25 +33,25 @@ def tile_picked_ydfm_lik_p_kernel(tc, x_words, x_scales, w1, w2, delay, elapsed,
         nc.sync.dma_start(offsets[:], offs)
 
         scale_table = keep.tile([P, T], U8, name="scale_table", align_bytes=64)
-        nc.gpsimd.memset(scale_table[:, : T // 2].bitcast(I32), 0)
-        nc.vector.memset(scale_table[:, T // 2 :].bitcast(I32), 0)
-        nc.scalar.dma_start(scale_table[32:96:4, :].bitcast(I32), x_scales[0].bitcast(I32))
+        nc.gpsimd.memset(scale_table[:, : 3 * T // 4].bitcast(I32), 0)
+        nc.vector.memset(scale_table[:, 3 * T // 4 :].bitcast(I32), 0)
+        nc.sync.dma_start(scale_table[32:96:4, :].bitcast(I32), x_scales[0].bitcast(I32))
         x_plane = keep.tile([P, S], U8, name="x_plane", align_bytes=64)
         nc.vector.memset(x_plane[:].bitcast(I32), 0)
 
         delay_col = keep.tile([P, 2], F32, name="delay_col")
         elapsed_col = keep.tile([P, 2], F32, name="elapsed_col")
-        nc.sync.dma_start(delay_col[:], delay[0].rearrange("(p j) -> p j", j=2))
-        nc.sync.dma_start(elapsed_col[:], elapsed[0].rearrange("(p j) -> p j", j=2))
+        nc.scalar.dma_start(delay_col[:], delay[0].rearrange("(p j) -> p j", j=2))
+        nc.scalar.dma_start(elapsed_col[:], elapsed[0].rearrange("(p j) -> p j", j=2))
         seen_sb = keep.tile([P, V], F32, name="seen_sb")
         nc.sync.dma_start(seen_sb[:], seen)
 
         w2_raw = keep.tile([P, PACK, N], F32, name="w2_raw")
         nc.sync.dma_start(w2_raw[:], w2.rearrange("(p j) n -> p j n", j=PACK))
-        w1_raw = keep.tile([P, PACK, N], F32, name="w1_raw")
-        nc.sync.dma_start(w1_raw[:], w1.rearrange("(p j) n -> p j n", j=PACK))
         word_table = keep.tile([P, T], I32, name="word_table", align_bytes=64)
         nc.sync.dma_start(word_table[:], x_words[0].rearrange("p c r -> p (c r)").bitcast(I32))
+        w1_raw = keep.tile([P, PACK, N], F32, name="w1_raw")
+        nc.sync.dma_start(w1_raw[:], w1.rearrange("(p j) n -> p j n", j=PACK))
 
         ident = keep.tile([P, P], F32, name="ident")
         make_identity(nc, ident[:])
@@ -100,7 +100,6 @@ def tile_picked_ydfm_lik_p_kernel(tc, x_words, x_scales, w1, w2, delay, elapsed,
             return codes, scales
 
         w2_q = quantize(w2_raw, "w2")
-        w1_q = quantize(w1_raw, "w1")
 
         picked = []
         for h in range(PIECES):
@@ -108,6 +107,8 @@ def tile_picked_ydfm_lik_p_kernel(tc, x_words, x_scales, w1, w2, delay, elapsed,
             cols = slice(h * PS // 16, (h + 1) * PS // 16)
             nc.vector.tensor_copy(words[:].rearrange("p d v -> p v d"), word_table[:].bitcast(U32).indirect(offsets[:, cols]))
             picked.append(words)
+
+        w1_q = quantize(w1_raw, "w1")
 
         def product(w_q, h, name):
             acc = psum.tile([P, PV], F32, name=name)
@@ -123,10 +124,8 @@ def tile_picked_ydfm_lik_p_kernel(tc, x_words, x_scales, w1, w2, delay, elapsed,
                 )
             return acc
 
-        h_sum, y_sum = [], []
-        for h in range(PIECES):
-            h_sum.append(product(w2_q, h, "h_sum%d" % h))
-            y_sum.append(product(w1_q, h, "y_sum%d" % h))
+        h_sum = [product(w2_q, h, "h_sum%d" % h) for h in range(PIECES)]
+        y_sum = [product(w1_q, h, "y_sum%d" % h) for h in range(PIECES)]
 
         def tiles(name):
             return [keep.tile([P, PV], F32, name="%s%d" % (name, h)) for h in range(PIECES)]
@@ -138,7 +137,6 @@ def tile_picked_ydfm_lik_p_kernel(tc, x_words, x_scales, w1, w2, delay, elapsed,
         for h in range(PIECES):
             nc.scalar.activation(lam[h][:], h_sum[h][:], ACT.Exp, scale=1.0 / D)
             nc.vector.scalar_tensor_tensor(seen_lh[h][:], h_sum[h][:], 1.0 / D, seen_sb[:, vs[h]], ALU.mult, ALU.mult)
-            nc.scalar.activation(th[h][:], y_sum[h][:], ACT.Tanh, scale=0.5 / D)
             nc.vector.tensor_tensor(
                 decay[h][:].rearrange("m (p j) -> m p j", j=2),
                 t_ps[:, :, h * PV // 2 : (h + 1) * PV // 2].rearrange("m j p -> m p j"),
@@ -147,6 +145,8 @@ def tile_picked_ydfm_lik_p_kernel(tc, x_words, x_scales, w1, w2, delay, elapsed,
             )
             nc.vector.tensor_tensor(z[h][:], seen_lh[h][:], decay[h][:], ALU.subtract)
             nc.scalar.activation(e[h][:], z[h][:], ACT.Exp)
+        for h in range(PIECES):
+            nc.scalar.activation(th[h][:], y_sum[h][:], ACT.Tanh, scale=0.5 / D)
             nc.vector.scalar_tensor_tensor(q[h][:], th[h][:], -1.0, neg_half_unseen[:, vs[h]], ALU.add, ALU.mult)
             nc.vector.scalar_tensor_tensor(r[h][:], th[h][:], 1.0, e[h][:], ALU.add, ALU.mult)
             nc.vector.scalar_tensor_tensor(res[h][:], r[h][:], 0.5, q[h][:], ALU.mult, ALU.add)

@@ -33,23 +33,24 @@ def tile_picked_ydfm_lik_p_kernel(tc, x_words, x_scales, w1, w2, delay, elapsed,
         nc.sync.dma_start(offsets[:], offs)
 
         scale_table = keep.tile([P, T], U8, name="scale_table", align_bytes=64)
-        nc.gpsimd.memset(scale_table[:, : 3 * T // 4].bitcast(I32), 0)
-        nc.vector.memset(scale_table[:, 3 * T // 4 :].bitcast(I32), 0)
-        nc.sync.dma_start(scale_table[32:96:4, :].bitcast(I32), x_scales[0].bitcast(I32))
+        nc.sync.dma_start(scale_table[16:32, :].bitcast(I32), x_scales[0].bitcast(I32))
+        nc.vector.memset(scale_table[0:16, :].bitcast(I32), 0)
+        nc.vector.memset(scale_table[32:64, :].bitcast(I32), 0)
+        nc.gpsimd.memset(scale_table[64:P, :].bitcast(I32), 0)
         x_plane = keep.tile([P, S], U8, name="x_plane", align_bytes=64)
-        nc.vector.memset(x_plane[:].bitcast(I32), 0)
+        nc.gpsimd.memset(x_plane[:].bitcast(I32), 0)
 
-        delay_col = keep.tile([P, 2], F32, name="delay_col")
-        elapsed_col = keep.tile([P, 2], F32, name="elapsed_col")
-        nc.scalar.dma_start(delay_col[:], delay[0].rearrange("(p j) -> p j", j=2))
-        nc.scalar.dma_start(elapsed_col[:], elapsed[0].rearrange("(p j) -> p j", j=2))
         seen_sb = keep.tile([P, V], F32, name="seen_sb")
         nc.sync.dma_start(seen_sb[:], seen)
 
-        w2_raw = keep.tile([P, PACK, N], F32, name="w2_raw")
-        nc.sync.dma_start(w2_raw[:], w2.rearrange("(p j) n -> p j n", j=PACK))
         word_table = keep.tile([P, T], I32, name="word_table", align_bytes=64)
         nc.sync.dma_start(word_table[:], x_words[0].rearrange("p c r -> p (c r)").bitcast(I32))
+        w2_raw = keep.tile([P, PACK, N], F32, name="w2_raw")
+        nc.sync.dma_start(w2_raw[:], w2.rearrange("(p j) n -> p j n", j=PACK))
+        delay_col = keep.tile([P, 2], F32, name="delay_col")
+        elapsed_col = keep.tile([P, 2], F32, name="elapsed_col")
+        nc.sync.dma_start(delay_col[:], delay[0].rearrange("(p j) -> p j", j=2))
+        nc.sync.dma_start(elapsed_col[:], elapsed[0].rearrange("(p j) -> p j", j=2))
         w1_raw = keep.tile([P, PACK, N], F32, name="w1_raw")
         nc.sync.dma_start(w1_raw[:], w1.rearrange("(p j) n -> p j n", j=PACK))
 
@@ -57,7 +58,7 @@ def tile_picked_ydfm_lik_p_kernel(tc, x_words, x_scales, w1, w2, delay, elapsed,
         make_identity(nc, ident[:])
 
         warm = keep.tile([P, 1], F32, name="warm")
-        nc.scalar.activation(warm[:], delay_col[:, 0:1], ACT.Exp, scale=-1.0)
+        nc.scalar.activation(warm[:], ident[:, 0:1], ACT.Exp)
 
         picked_scales = keep.tile([P, S], U8, name="picked_scales", align_bytes=64)
         nc.vector.tensor_copy(picked_scales[:], scale_table[:].indirect(offsets[:]))
@@ -67,7 +68,19 @@ def tile_picked_ydfm_lik_p_kernel(tc, x_words, x_scales, w1, w2, delay, elapsed,
             picked_scales[:].rearrange("p (h v d) -> p h d v", h=PIECES, d=D),
         )
         for i in range(4):
-            nc.sync.dma_start(x_plane[i:P:32, :].bitcast(I32), dealt_scales[32 + 4 * i : 96 : 16, :].bitcast(I32))
+            nc.sync.dma_start(x_plane[i:P:32, :].bitcast(I32), dealt_scales[16 + i : 32 : 4, :].bitcast(I32))
+
+        def quantize(raw, name, tag):
+            grouped = keep.tile([P, N, PACK], BF16, name=name + "_grouped", tag=tag, align_bytes=64)
+            codes = keep.tile([P, N], U32, name=name + "_codes", align_bytes=64)
+            scales = keep.tile([P, N], U8, name=name + "_scales", align_bytes=64)
+            nc.scalar.copy(
+                grouped[:].rearrange("p (c i) t -> p c t i", i=4), raw[:].rearrange("p t (c i) -> p c t i", i=4)
+            )
+            nc.vector.quantize_mx(codes[:].bitcast(FP8X4), scales[:], grouped[:].rearrange("p n t -> p (n t)"))
+            return codes, scales
+
+        w2_q = quantize(w2_raw, "w2", "piece1")
 
         neg_elapsed_col = keep.tile([P, 2], F32, name="neg_elapsed_col")
         nc.scalar.mul(neg_elapsed_col[:], elapsed_col[:], -1.0)
@@ -89,26 +102,14 @@ def tile_picked_ydfm_lik_p_kernel(tc, x_words, x_scales, w1, w2, delay, elapsed,
         neg_half_unseen = keep.tile([P, V], F32, name="neg_half_unseen")
         nc.scalar.activation(neg_half_unseen[:], seen_sb[:], ACT.Copy, scale=0.5, bias=-0.5)
 
-        def quantize(raw, name):
-            grouped = keep.tile([P, N, PACK], BF16, name=name + "_grouped", align_bytes=64)
-            codes = keep.tile([P, N], U32, name=name + "_codes", align_bytes=64)
-            scales = keep.tile([P, N], U8, name=name + "_scales", align_bytes=64)
-            nc.scalar.copy(
-                grouped[:].rearrange("p (c i) t -> p c t i", i=4), raw[:].rearrange("p t (c i) -> p c t i", i=4)
-            )
-            nc.vector.quantize_mx(codes[:].bitcast(FP8X4), scales[:], grouped[:].rearrange("p n t -> p (n t)"))
-            return codes, scales
-
-        w2_q = quantize(w2_raw, "w2")
-
         picked = []
         for h in range(PIECES):
-            words = keep.tile([P, D, PV], U32, name="picked_words%d" % h, align_bytes=64)
+            words = keep.tile([P, D, PV], U32, name="picked_words%d" % h, tag="piece%d" % h, align_bytes=64)
             cols = slice(h * PS // 16, (h + 1) * PS // 16)
             nc.vector.tensor_copy(words[:].rearrange("p d v -> p v d"), word_table[:].bitcast(U32).indirect(offsets[:, cols]))
             picked.append(words)
 
-        w1_q = quantize(w1_raw, "w1")
+        w1_q = quantize(w1_raw, "w1", "w1_grouped")
 
         def product(w_q, h, name):
             acc = psum.tile([P, PV], F32, name=name)
@@ -134,20 +135,27 @@ def tile_picked_ydfm_lik_p_kernel(tc, x_words, x_scales, w1, w2, delay, elapsed,
             tiles(n) for n in ("lam", "seen_lh", "decay", "z", "e", "th", "q", "r", "res")
         ]
         vs = [slice(h * PV, (h + 1) * PV) for h in range(PIECES)]
+        strips = [[(0, PV)], [(0, PV // 2), (PV // 2, PV)]]
         for h in range(PIECES):
-            nc.scalar.activation(lam[h][:], h_sum[h][:], ACT.Exp, scale=1.0 / D)
+            for lo, hi in strips[h]:
+                nc.scalar.activation(lam[h][:, lo:hi], h_sum[h][:, lo:hi], ACT.Exp, scale=1.0 / D)
+            for lo, hi in strips[h]:
+                nc.vector.tensor_tensor(
+                    decay[h][:, lo:hi].rearrange("m (p j) -> m p j", j=2),
+                    t_ps[:, :, (h * PV + lo) // 2 : (h * PV + hi) // 2].rearrange("m j p -> m p j"),
+                    lam[h][:, lo:hi].rearrange("m (p j) -> m p j", j=2),
+                    ALU.mult,
+                )
             nc.vector.scalar_tensor_tensor(seen_lh[h][:], h_sum[h][:], 1.0 / D, seen_sb[:, vs[h]], ALU.mult, ALU.mult)
-            nc.vector.tensor_tensor(
-                decay[h][:].rearrange("m (p j) -> m p j", j=2),
-                t_ps[:, :, h * PV // 2 : (h + 1) * PV // 2].rearrange("m j p -> m p j"),
-                lam[h][:].rearrange("m (p j) -> m p j", j=2),
-                ALU.mult,
-            )
-            nc.vector.tensor_tensor(z[h][:], seen_lh[h][:], decay[h][:], ALU.subtract)
-            nc.scalar.activation(e[h][:], z[h][:], ACT.Exp)
+            for lo, hi in strips[h]:
+                nc.vector.tensor_tensor(z[h][:, lo:hi], seen_lh[h][:, lo:hi], decay[h][:, lo:hi], ALU.subtract)
+            for lo, hi in strips[h]:
+                nc.scalar.activation(e[h][:, lo:hi], z[h][:, lo:hi], ACT.Exp)
         for h in range(PIECES):
             nc.scalar.activation(th[h][:], y_sum[h][:], ACT.Tanh, scale=0.5 / D)
             nc.vector.scalar_tensor_tensor(q[h][:], th[h][:], -1.0, neg_half_unseen[:, vs[h]], ALU.add, ALU.mult)
-            nc.vector.scalar_tensor_tensor(r[h][:], th[h][:], 1.0, e[h][:], ALU.add, ALU.mult)
-            nc.vector.scalar_tensor_tensor(res[h][:], r[h][:], 0.5, q[h][:], ALU.mult, ALU.add)
+            for lo, hi in strips[h]:
+                nc.vector.scalar_tensor_tensor(r[h][:, lo:hi], th[h][:, lo:hi], 1.0, e[h][:, lo:hi], ALU.add, ALU.mult)
+            for lo, hi in strips[h]:
+                nc.vector.scalar_tensor_tensor(res[h][:, lo:hi], r[h][:, lo:hi], 0.5, q[h][:, lo:hi], ALU.mult, ALU.add)
             nc.sync.dma_start(out[:, vs[h]], res[h][:])

from contextlib import ExitStack

import concourse.mybir as mybir
from concourse.masks import make_identity

F32 = mybir.dt.float32
BF16 = mybir.dt.bfloat16
I32 = mybir.dt.int32
U32 = mybir.dt.uint32
U16 = mybir.dt.uint16
U8 = mybir.dt.uint8
FP8X4 = mybir.dt.float8_e4m3fn_x4
ALU = mybir.AluOpType
ACT = mybir.ActivationFunctionType

P = 128
K, T, S, D, N, V = 512, 4096, 1024, 4, 128, 256
PACK = 4
PIECES = 2
PV = V // PIECES
PS = S // PIECES

FLOPS = 2 * 2 * K * N * S


def tile_picked_ydfm_lik_p_kernel(tc, x_words, x_scales, w1, w2, delay, elapsed, seen, offs, out):
    nc = tc.nc
    with ExitStack() as ctx:
        keep = ctx.enter_context(tc.tile_pool(name="keep", bufs=1))
        psum = ctx.enter_context(tc.psum_pool(name="psum", bufs=1))

        offsets = keep.tile([P, S // 16], U16, name="offsets")
        nc.sync.dma_start(offsets[:], offs)

        scale_table = keep.tile([P, T], U8, name="scale_table", align_bytes=64)
        nc.sync.dma_start(scale_table[16:32, :].bitcast(I32), x_scales[0].bitcast(I32))
        nc.vector.memset(scale_table[0:16, :].bitcast(I32), 0)
        nc.vector.memset(scale_table[32:64, :].bitcast(I32), 0)
        nc.gpsimd.memset(scale_table[64:P, :].bitcast(I32), 0)
        x_plane = keep.tile([P, S], U8, name="x_plane", align_bytes=64)
        nc.gpsimd.memset(x_plane[:].bitcast(I32), 0)

        seen_sb = keep.tile([P, V], F32, name="seen_sb")
        nc.sync.dma_start(seen_sb[:], seen)

        word_table = keep.tile([P, T], I32, name="word_table", align_bytes=64)
        nc.sync.dma_start(word_table[:], x_words[0].rearrange("p c r -> p (c r)").bitcast(I32))
        w2_raw = keep.tile([P, PACK, N], F32, name="w2_raw")
        nc.sync.dma_start(w2_raw[:], w2.rearrange("(p j) n -> p j n", j=PACK))
        delay_col = keep.tile([P, 2], F32, name="delay_col")
        elapsed_col = keep.tile([P, 2], F32, name="elapsed_col")
        nc.sync.dma_start(delay_col[:], delay[0].rearrange("(p j) -> p j", j=2))
        nc.sync.dma_start(elapsed_col[:], elapsed[0].rearrange("(p j) -> p j", j=2))
        w1_raw = keep.tile([P, PACK, N], F32, name="w1_raw")
        nc.sync.dma_start(w1_raw[:], w1.rearrange("(p j) n -> p j n", j=PACK))

        ident = keep.tile([P, P], F32, name="ident")
        make_identity(nc, ident[:])

        warm = keep.tile([P, 1], F32, name="warm")
        nc.scalar.activation(warm[:], ident[:, 0:1], ACT.Exp)

        picked_scales = keep.tile([P, S], U8, name="picked_scales", align_bytes=64)
        nc.vector.tensor_copy(picked_scales[:], scale_table[:].indirect(offsets[:]))
        dealt_scales = keep.tile([P, S], U8, name="dealt_scales", align_bytes=64)
        nc.vector.tensor_copy(
            dealt_scales[:].rearrange("p (h d v) -> p h d v", h=PIECES, d=D),
            picked_scales[:].rearrange("p (h v d) -> p h d v", h=PIECES, d=D),
        )
        for i in range(4):
            nc.sync.dma_start(x_plane[i:P:32, :].bitcast(I32), dealt_scales[16 + i : 32 : 4, :].bitcast(I32))

        def quantize(raw, name, tag):
            grouped = keep.tile([P, N, PACK], BF16, name=name + "_grouped", tag=tag, align_bytes=64)
            codes = keep.tile([P, N], U32, name=name + "_codes", align_bytes=64)
            scales = keep.tile([P, N], U8, name=name + "_scales", align_bytes=64)
            nc.scalar.copy(
                grouped[:].rearrange("p (c i) t -> p c t i", i=4), raw[:].rearrange("p t (c i) -> p c t i", i=4)
            )
            nc.vector.quantize_mx(codes[:].bitcast(FP8X4), scales[:], grouped[:].rearrange("p n t -> p (n t)"))
            return codes, scales

        w2_q = quantize(w2_raw, "w2", "piece1")

        neg_elapsed_col = keep.tile([P, 2], F32, name="neg_elapsed_col")
        nc.scalar.mul(neg_elapsed_col[:], elapsed_col[:], -1.0)
        seen_t = psum.tile([P, 2, P], F32, name="seen_t")
        for j in range(2):
            nc.tensor.transpose(seen_t[:, j, :], seen_sb[:, j:V:2], ident[:])
        seen_delay = keep.tile([P, 2, P], F32, name="seen_delay")
        unseen_elapsed = keep.tile([P, 2, P], F32, name="unseen_elapsed")
        t_ps = psum.tile([P, 2, P], F32, name="t_ps")
        for j in range(2):
            nc.scalar.activation(seen_delay[:, j, :], seen_t[:, j, :], ACT.Copy, scale=delay_col[:, j : j + 1])
            nc.scalar.activation(
                unseen_elapsed[:, j, :], seen_t[:, j, :], ACT.Identity,
                scale=neg_elapsed_col[:, j : j + 1], bias=elapsed_col[:, j : j + 1],
            )
        for j in range(2):
            nc.tensor.matmul(t_ps[:, j, :], seen_delay[:, j, :], ident[:], start=True, stop=False, is_transpose=True)
            nc.tensor.matmul(t_ps[:, j, :], unseen_elapsed[:, j, :], ident[:], start=False, stop=True, is_transpose=True)
        neg_half_unseen = keep.tile([P, V], F32, name="neg_half_unseen")
        nc.scalar.activation(neg_half_unseen[:], seen_sb[:], ACT.Copy, scale=0.5, bias=-0.5)

        picked = []
        for h in range(PIECES):
            words = keep.tile([P, D, PV], U32, name="picked_words%d" % h, tag="piece%d" % h, align_bytes=64)
            cols = slice(h * PS // 16, (h + 1) * PS // 16)
            nc.vector.tensor_copy(words[:].rearrange("p d v -> p v d"), word_table[:].bitcast(U32).indirect(offsets[:, cols]))
            picked.append(words)

        w1_q = quantize(w1_raw, "w1", "w1_grouped")

        def product(w_q, h, name):
            acc = psum.tile([P, PV], F32, name=name)
            for d in range(D):
                nc.tensor.matmul_mx(
                    acc[:],
                    lhsT=w_q[0][:].bitcast(FP8X4),
                    lhsT_scale=w_q[1][:],
                    rhs=picked[h][:, d, :].bitcast(FP8X4),
                    rhs_scale=x_plane[:, (h * D + d) * PV : (h * D + d + 1) * PV],
                    start=(d == 0),
                    stop=(d == D - 1),
                )
            return acc

        h_sum = [product(w2_q, h, "h_sum%d" % h) for h in range(PIECES)]
        y_sum = [product(w1_q, h, "y_sum%d" % h) for h in range(PIECES)]

        def tiles(name):
            return [keep.tile([P, PV], F32, name="%s%d" % (name, h)) for h in range(PIECES)]

        lam, seen_lh, decay, z, e, th, q, r, res = [
            tiles(n) for n in ("lam", "seen_lh", "decay", "z", "e", "th", "q", "r", "res")
        ]
        vs = [slice(h * PV, (h + 1) * PV) for h in range(PIECES)]
        strips = [[(0, PV)], [(0, PV // 2), (PV // 2, PV)]]
        for h in range(PIECES):
            for lo, hi in strips[h]:
                nc.scalar.activation(lam[h][:, lo:hi], h_sum[h][:, lo:hi], ACT.Exp, scale=1.0 / D)
            for lo, hi in strips[h]:
                nc.vector.tensor_tensor(
                    decay[h][:, lo:hi].rearrange("m (p j) -> m p j", j=2),
                    t_ps[:, :, (h * PV + lo) // 2 : (h * PV + hi) // 2].rearrange("m j p -> m p j"),
                    lam[h][:, lo:hi].rearrange("m (p j) -> m p j", j=2),
                    ALU.mult,
                )
            nc.vector.scalar_tensor_tensor(seen_lh[h][:], h_sum[h][:], 1.0 / D, seen_sb[:, vs[h]], ALU.mult, ALU.mult)
            for lo, hi in strips[h]:
                nc.vector.tensor_tensor(z[h][:, lo:hi], seen_lh[h][:, lo:hi], decay[h][:, lo:hi], ALU.subtract)
            for lo, hi in strips[h]:
                nc.scalar.activation(e[h][:, lo:hi], z[h][:, lo:hi], ACT.Exp)
        for h in range(PIECES):
            nc.scalar.activation(th[h][:], y_sum[h][:], ACT.Tanh, scale=0.5 / D)
            nc.vector.scalar_tensor_tensor(q[h][:], th[h][:], -1.0, neg_half_unseen[:, vs[h]], ALU.add, ALU.mult)
            for lo, hi in strips[h]:
                nc.vector.scalar_tensor_tensor(r[h][:, lo:hi], th[h][:, lo:hi], 1.0, e[h][:, lo:hi], ALU.add, ALU.mult)
            for lo, hi in strips[h]:
                nc.vector.scalar_tensor_tensor(res[h][:, lo:hi], r[h][:, lo:hi], 0.5, q[h][:, lo:hi], ALU.mult, ALU.add)
            nc.sync.dma_start(out[:, vs[h]], res[h][:])
